import numpy as np
import ml_dtypes


def mxq(x, axis, fmt="e4m3"):
    dtype, down = {"e4m3": (ml_dtypes.float8_e4m3fn, 7), "e5m2": (ml_dtypes.float8_e5m2, 14)}[fmt]
    v = np.moveaxis(np.asarray(x, np.float32).astype(ml_dtypes.bfloat16).astype(np.float64), axis, -1)
    blocks = v.reshape(v.shape[:-1] + (-1, 32))
    amax = np.abs(blocks).max(-1, keepdims=True)
    byte = np.maximum(np.where(amax > 0, np.frexp(amax)[1] - 1 + 127, 0) - down, 1)
    scale = np.exp2(byte - 127.0)
    codes = (blocks / scale).astype(np.float32).astype(dtype).astype(np.float64)
    return np.moveaxis((codes * scale).reshape(v.shape), -1, axis)


WIDE = False


def mx_kscale(k):
    if not WIDE:
        return np.ones(k)
    levels = np.array([10, -10, 5, -5, 0])
    if k % 512:
        return np.exp2(np.random.permutation(np.resize(levels, k // 32))).repeat(32)
    a = np.empty((k // 512, 16))
    for p in range(k // 512):
        a[p, :8] = np.random.permutation(np.resize(levels, 8))
        for g in range(8):
            far = levels[np.abs(levels - a[p, g]) >= 10]
            a[p, g + 8] = far[np.random.randint(len(far))]
    return np.exp2(a.ravel()).repeat(32)


def f64(x):
    return np.asarray(x).astype(np.float64)


def striped(idx):
    return np.tile(np.asarray(idx).reshape(-1, 16).T, (8, 1)).astype(np.uint16)


def unstriped(offs):
    return offs[:16].T.reshape(-1).astype(np.int64)


E2M1 = np.array([0.0, 0.5, 1.0, 1.5, 2.0, 3.0, 4.0, 6.0, -0.0, -0.5, -1.0, -1.5, -2.0, -3.0, -4.0, -6.0])


def pack_weight(w, fmt):
    k, n = w.shape
    w = f64(np.asarray(w, np.float32).astype(ml_dtypes.bfloat16)).reshape(k // 32, 32, n)
    amax = np.abs(w).max(1)
    if fmt == "e4m3":
        byte = np.frexp(amax)[1] - 1 + 127 - 7
    else:
        mant, ex = np.frexp(amax / 6.0)
        byte = np.where(mant > 0.5, ex, ex - 1) + 127
    byte = np.clip(np.where(amax > 0, byte, 1), 1, 254)
    scaled = (w * np.exp2(127.0 - byte)[:, None, :]).reshape(k, n).astype(np.float32)
    by_word = np.ascontiguousarray(scaled.reshape(k // 512, 128, 4, n).transpose(0, 1, 3, 2))
    if fmt == "e4m3":
        words = by_word.astype(ml_dtypes.float8_e4m3fn).view(np.uint8)
    else:
        c = by_word.astype(ml_dtypes.float4_e2m1fn).view(np.uint8) & 0xF
        words = (c[..., 0::2] | (c[..., 1::2] << 4)).reshape(k // 512, 128, 2 * n)
    return np.ascontiguousarray(words), np.ascontiguousarray(byte.astype(np.uint8).reshape(k // 512, 16, n))


def unpack_weight(words, scales, fmt):
    g, _, n = scales.shape
    words = np.ascontiguousarray(words).reshape(g, 128, n, -1)
    if fmt == "e4m3":
        vals = words.view(ml_dtypes.float8_e4m3fn).astype(np.float64)
    else:
        nib = np.empty((g, 128, n, 4), np.uint8)
        nib[..., 0::2] = words & 0xF
        nib[..., 1::2] = words >> 4
        vals = E2M1[nib]
    vals = vals * np.repeat(np.exp2(scales.astype(np.float64) - 127.0), 8, axis=1)[..., None]
    return vals.transpose(0, 1, 3, 2).reshape(g * 512, n)


D, T, I, Q, E, Z, M = 512, 2048, 512, 256, 512, 1024, 1024


def setup_inputs():
    n = np.random.standard_normal
    idx = np.random.permutation(T)[:I]
    idx2 = np.random.permutation(Z)[:I]
    idx3 = np.random.permutation(M)[:Q]
    fd = mx_kscale(D)
    fi = mx_kscale(I)
    ti = np.ones(T)
    ti[idx] = fi
    keysp = pack_weight(n((D, T)) / fd[:, None], "e4m3")
    return {
        "query": (n((D, Q)) * 1.0 / np.sqrt(D) * fd[:, None]).astype(np.float32),
        "keys_words": keysp[0],
        "keys_scales": keysp[1],
        "earl": (np.random.uniform(0.3, 1.7, (Q, Z))).astype(np.float32),
        "os": (np.random.uniform(0.02, 0.08, (1, I)) * fi).astype(np.float32),
        "vals": (n((E, T)) / ti).astype(np.float32),
        "old": (n((E, M)) * 2.0).astype(np.float32),
        "fade": (np.random.uniform(0.3, 0.9, (1, M))).astype(np.float32),
        "offs": striped(idx),
        "offs2": striped(idx2),
        "offs3": striped(idx3),
    }


def reference(query, keys_words, keys_scales, earl, os, vals, old, fade, offs, offs2, offs3):
    idx = unstriped(offs)
    idx2 = unstriped(offs2)
    idx3 = unstriped(offs3)
    keysu = unpack_weight(keys_words, keys_scales, "e4m3")
    queryq = mxq(f64(query), 0, "e4m3")
    keysidxg = keysu[:, idx]
    a = queryq.T @ keysidxg
    w = a * f64(earl)[:, idx2]
    wo1 = w * f64(os)
    wt1 = wo1.T
    vt1 = f64(vals)[:, idx].T
    vt1q = mxq(vt1, 0, "e4m3")
    wt1q = mxq(wt1, 0, "e4m3")
    o = vt1q.T @ wt1q
    of = np.zeros((E, M))
    of[:, idx3] = o
    y = f64(old) * f64(fade) + of
    return y

@@ -1,0 +1,208 @@
+from contextlib import ExitStack
+
+import concourse.mybir as mybir
+from concourse.masks import make_identity
+
+F32 = mybir.dt.float32
+BF16 = mybir.dt.bfloat16
+U32 = mybir.dt.uint32
+I32 = mybir.dt.int32
+U16 = mybir.dt.uint16
+U8 = mybir.dt.uint8
+FP8X4 = mybir.dt.float8_e4m3fn_x4
+MULT = mybir.AluOpType.mult
+ADD = mybir.AluOpType.add
+COPY = mybir.ActivationFunctionType.Copy
+
+D, T, I, Q, E, Z, M = 512, 2048, 512, 256, 512, 1024, 1024
+P = 128
+PACK = 4
+BANK = 512
+Q_TILES = Q // P
+E_TILES = E // P
+M_BANKS = M // BANK
+
+LOADS = (("o", 0), ("v", 1), ("o", 1), ("v", 2), ("v", 3), ("o", 2), ("o", 3),)
+TEXT = (("A", 0), ("A", 1), ("B", 0), ("M", 0), ("A", 2), ("B", 1), ("A", 3), ("C", 0), ("B", 2), ("M", 1), ("C", 1), ("B", 3), ("M", 2), ("C", 2), ("M", 3), ("C", 3),)
+VG = "SSVV"
+VBF = "VVVV"
+OC = "SSSS"
+SC = "SSSS"
+ADDE = "GGVV"
+OTAG = ["vals1","vals2","o2","o3"]
+RTAG = ["r0","r1","r2","r3"]
+SPLIT = [2,3]
+
+FLOPS = 2 * D * Q * I + 2 * I * E * Q
+
+
+def tile_attend_earliertable_written_lean_kernel(
+    tc, query, keys_words, keys_scales, earl, slot_factor, vals, old, fade, offs, offs2, offs3, out
+):
+    nc = tc.nc
+    with ExitStack() as ctx:
+        keep = ctx.enter_context(tc.tile_pool(name="keep", bufs=1))
+        psum = ctx.enter_context(tc.psum_pool(name="psum", bufs=1))
+
+        tok_list = keep.tile([P, I // 16], U16, name="tok_list")
+        earl_list = keep.tile([P, I // 16], U16, name="earl_list")
+        col_list = keep.tile([P, Q // 16], U16, name="col_list")
+        key_words = keep.tile([P, T], U32, name="key_words")
+        key_bytes = keep.tile([P, T], U8, name="key_bytes")
+        q_raw = [keep.tile([P, PACK, P], F32, name=f"q_raw{h}") for h in range(Q_TILES)]
+        earl_sb = [keep.tile([P, Z], F32, name=f"earl_sb{h}") for h in range(Q_TILES)]
+        vals_sb = [keep.tile([P, T], F32, name=f"vals_sb{c}", tag=f"vals{c}", align_bytes=64) for c in range(E_TILES)]
+        old_sb = [keep.tile([P, M], F32, name=f"old_sb{c}") for c in range(E_TILES)]
+        factor_sb = keep.tile([P, PACK], F32, name="factor_sb")
+        fade_sb = keep.tile([P, M_BANKS, PACK], F32, name="fade_sb")
+        ident = keep.tile([P, P], F32, name="ident")
+        placed = [keep.tile([P, M], F32, name=f"placed{c}") for c in range(E_TILES)]
+
+        nc.vector.memset(key_bytes[:].bitcast(I32), 0)
+        make_identity(nc, ident[:])
+        nc.gpsimd.dma_start(factor_sb[:], slot_factor[0].rearrange("(p t) -> p t", t=PACK))
+        nc.gpsimd.dma_start(fade_sb[:], fade[0].rearrange("(b p j) -> p b j", b=M_BANKS, j=PACK))
+
+        nc.sync.dma_start(tok_list[:], offs)
+        nc.sync.dma_start(earl_list[:], offs2)
+        nc.sync.dma_start(earl_sb[0][:], earl[0:P, :])
+        for quad in range(4):
+            nc.scalar.dma_start(
+                key_bytes[32 * quad : 32 * quad + 4, :].bitcast(I32),
+                keys_scales[0, 4 * quad : 4 * quad + 4, :].bitcast(I32),
+            )
+        nc.sync.dma_start(key_words[:].bitcast(I32), keys_words[0].rearrange("p n t -> p (n t)").bitcast(I32))
+        nc.sync.dma_start(earl_sb[1][:], earl[P : 2 * P, :])
+        for h in range(Q_TILES):
+            nc.sync.dma_start(q_raw[h][:], query.rearrange("(p j) q -> p j q", j=PACK)[:, :, h * P : (h + 1) * P])
+        nc.sync.dma_start(vals_sb[0][:], vals[0:P, :])
+        nc.sync.dma_start(col_list[:], offs3)
+        for kind, c in LOADS:
+            if kind == "v":
+                nc.sync.dma_start(vals_sb[c][:], vals[c * P : (c + 1) * P, :])
+            else:
+                nc.sync.dma_start(old_sb[c][:], old[c * P : (c + 1) * P, :])
+
+        for c in range(E_TILES):
+            nc.vector.memset(placed[c][:], 0.0)
+
+        kg_words = keep.tile([P, I], U32, name="kg_words", align_bytes=64)
+        kg_bytes = keep.tile([P, I], U8, name="kg_bytes", align_bytes=64)
+        nc.vector.tensor_copy(kg_bytes[:].rearrange("p (t s) -> p s t", t=PACK), key_bytes[:].indirect(tok_list[:]))
+        nc.vector.tensor_copy(kg_words[:].rearrange("p (t s) -> p s t", t=PACK), key_words[:].indirect(tok_list[:]))
+
+        gain = keep.tile([P, Q_TILES, PACK, P], F32, name="gain")
+        for h in range(Q_TILES):
+            eg = keep.tile([P, I], F32, name=f"eg{h}")
+            nc.scalar.activation(eg[:], earl_sb[h][:].indirect(earl_list[:]), COPY)
+            turned = psum.tile([P, PACK, P], F32, name="turned", tag=f"turn{h}")
+            for t in range(PACK):
+                nc.tensor.transpose(turned[:, t, :], eg[:, t::PACK], ident[:])
+            for t in range(PACK):
+                nc.scalar.activation(gain[:, h, t, :], turned[:, t, :], COPY, scale=factor_sb[:, t : t + 1])
+
+        q_bf = keep.tile([P, Q, PACK], BF16, name="q_bf", align_bytes=64)
+        q_codes = keep.tile([P, Q], U32, name="q_codes", align_bytes=64)
+        q_scales = keep.tile([P, Q], U8, name="q_scales", align_bytes=64)
+        for h in range(Q_TILES):
+            rows = slice(h * P, (h + 1) * P)
+            nc.vector.tensor_copy(q_bf[:, rows, :], q_raw[h][:].rearrange("p j q -> p q j"))
+            nc.vector.quantize_mx(
+                out=q_codes[:, rows].bitcast(FP8X4), scales=q_scales[:, rows], in_=q_bf[:, rows, :].rearrange("p q j -> p (q j)")
+            )
+
+        w_bf = keep.tile([P, Q, PACK], BF16, name="w_bf", align_bytes=64)
+        w_codes = keep.tile([P, Q], U32, name="w_codes", align_bytes=64)
+        w_scales = keep.tile([P, Q], U8, name="w_scales", align_bytes=64)
+        for h in range(Q_TILES):
+            rows = slice(h * P, (h + 1) * P)
+            scores = psum.tile([P, PACK, P], F32, name="scores", tag=f"acc{h}")
+            for t in range(PACK):
+                cols = slice(t * P, (t + 1) * P)
+                nc.tensor.matmul_mx(
+                    out=scores[:, t, :],
+                    lhsT=kg_words[:, cols].bitcast(FP8X4),
+                    lhsT_scale=kg_bytes[:, cols],
+                    rhs=q_codes[:, rows].bitcast(FP8X4),
+                    rhs_scale=q_scales[:, rows],
+                    start=True,
+                    stop=True,
+                )
+            nc.vector.tensor_tensor(
+                w_bf[:, rows, :], scores[:].rearrange("p t q -> p q t"), gain[:, h].rearrange("p t q -> p q t"), MULT
+            )
+        nc.vector.quantize_mx(out=w_codes[:].bitcast(FP8X4), scales=w_scales[:], in_=w_bf[:].rearrange("p q j -> p (q j)"))
+
+        fade_ps = [psum.tile([P, PACK, P], F32, name=f"fade_ps{b}") for b in range(M_BANKS)]
+        for b in range(M_BANKS):
+            for j in range(PACK):
+                nc.tensor.transpose(fade_ps[b][:, j, :], fade_sb[:, b, j : j + 1].to_broadcast([P, P]), ident[:])
+
+        v_codes = [keep.tile([P, P], U32, name=f"v_codes{c}", align_bytes=64) for c in range(E_TILES)]
+        v_scales = [keep.tile([P, P], U8, name=f"v_scales{c}", align_bytes=64) for c in range(E_TILES)]
+        faded = [keep.tile([P, M], F32, name=f"faded{c}") for c in range(E_TILES)]
+
+        def copy_on(eng, dst, src):
+            if eng == "S":
+                nc.scalar.copy(dst, src)
+            else:
+                nc.vector.tensor_copy(dst, src)
+
+        def indirect_on(eng, dst, src):
+            if eng == "S":
+                nc.scalar.activation(dst, src, COPY)
+            else:
+                nc.vector.tensor_copy(dst, src)
+
+        def values(c):
+            vg = keep.tile([P, I], BF16, name=f"vg{c}")
+            indirect_on(VG[c], vg[:], vals_sb[c][:].indirect(tok_list[:]))
+            pairs = vg[:].bitcast(F32)
+            v_turned = psum.tile([P, 2, P], F32, name="v_turned", tag=f"turn{c % 2}")
+            for u in range(2):
+                nc.tensor.transpose(v_turned[:, u, :], pairs[:, u::2], ident[:])
+            v_bf = keep.tile([P, P, PACK], BF16, name=f"v_bf{c}", tag=f"v_bf{c}", align_bytes=64)
+            copy_on(VBF[c], v_bf[:].bitcast(F32), v_turned[:].rearrange("p u e -> p e u"))
+            nc.vector.quantize_mx(
+                out=v_codes[c][:].bitcast(FP8X4), scales=v_scales[c][:], in_=v_bf[:].rearrange("p e j -> p (e j)")
+            )
+
+        def product(c):
+            o_ps = psum.tile([P, Q], F32, name="o_ps", tag=f"acc{c % 2}")
+            nc.tensor.matmul_mx(
+                out=o_ps[:],
+                lhsT=v_codes[c][:].bitcast(FP8X4),
+                lhsT_scale=v_scales[c][:],
+                rhs=w_codes[:].bitcast(FP8X4),
+                rhs_scale=w_scales[:],
+                start=True,
+                stop=True,
+            )
+            o_sb = keep.tile([P, Q], F32, name=f"o_sb{c}", tag=OTAG[c], align_bytes=64)
+            copy_on(OC[c], o_sb[:], o_ps[:])
+            indirect_on(SC[c], placed[c][:].indirect(col_list[:]), o_sb[:])
+
+        def fading(c):
+            for b in range(M_BANKS):
+                cols = slice(b * BANK, (b + 1) * BANK)
+                nc.vector.tensor_tensor(
+                    faded[c][:, cols].rearrange("p (r j) -> p r j", j=PACK),
+                    old_sb[c][:, cols].rearrange("p (r j) -> p r j", j=PACK),
+                    fade_ps[b][:].rearrange("p j r -> p r j"),
+                    MULT,
+                )
+
+        def finish(c):
+            result = keep.tile([P, M], F32, name=f"result{c}", tag=RTAG[c], align_bytes=64)
+            eng = nc.gpsimd if ADDE[c] == "G" else nc.vector
+            for b in range(M_BANKS):
+                cols = slice(b * BANK, (b + 1) * BANK)
+                eng.tensor_tensor(result[:, cols], faded[c][:, cols], placed[c][:, cols], ADD)
+                if c in SPLIT:
+                    nc.sync.dma_start(out[c * P : (c + 1) * P, cols], result[:, cols])
+            if c not in SPLIT:
+                nc.sync.dma_start(out[c * P : (c + 1) * P, :], result[:])
+
+        steps = {"A": values, "B": product, "M": fading, "C": finish}
+        for kind, c in TEXT:
+            steps[kind](c)

@@ -22,17 +22,18 @@ Q_TILES = Q // P
 E_TILES = E // P
 M_BANKS = M // BANK
 
-LOADS = (("o", 0), ("v", 1), ("o", 1), ("v", 2), ("v", 3), ("o", 2), ("o", 3),)
-TEXT = (("A", 0), ("A", 1), ("B", 0), ("M", 0), ("A", 2), ("B", 1), ("A", 3), ("C", 0), ("B", 2), ("M", 1), ("C", 1), ("B", 3), ("M", 2), ("C", 2), ("M", 3), ("C", 3),)
-VG = "SSVV"
+LOADS = (("v", 0), ("v", 1), ("l", 0), ("o", 0), ("v", 2), ("o", 1), ("v", 3), ("o", 2), ("o", 3),)
+TEXT = (("A", 0), ("A", 1), ("B", 0), ("M", 0), ("A", 2), ("B", 1), ("C", 0), ("A", 3), ("B", 2), ("M", 1), ("C", 1), ("B", 3), ("M", 2), ("C", 2), ("M", 3), ("C", 3),)
+VG = "SSSS"
 VBF = "VVVV"
 OC = "SSSS"
 SC = "SSSS"
-ADDE = "GGVV"
-OTAG = ["vals1","vals2","o2","o3"]
+ADDE = "VVVV"
+OTAG = ["vals1","vals2","vals3","o3"]
 RTAG = ["r0","r1","r2","r3"]
-SPLIT = [2,3]
+PIECES = [1,1,2,2]
 
+WINDOWS = 2
 FLOPS = 2 * D * Q * I + 2 * I * E * Q
 
 
@@ -49,41 +50,40 @@ def tile_attend_earliertable_written_lean_kernel(
         col_list = keep.tile([P, Q // 16], U16, name="col_list")
         key_words = keep.tile([P, T], U32, name="key_words")
         key_bytes = keep.tile([P, T], U8, name="key_bytes")
-        q_raw = [keep.tile([P, PACK, P], F32, name=f"q_raw{h}") for h in range(Q_TILES)]
+        q_raw = keep.tile([P, PACK, Q], F32, name="q_raw")
         earl_sb = [keep.tile([P, Z], F32, name=f"earl_sb{h}") for h in range(Q_TILES)]
         vals_sb = [keep.tile([P, T], F32, name=f"vals_sb{c}", tag=f"vals{c}", align_bytes=64) for c in range(E_TILES)]
         old_sb = [keep.tile([P, M], F32, name=f"old_sb{c}") for c in range(E_TILES)]
         factor_sb = keep.tile([P, PACK], F32, name="factor_sb")
         fade_sb = keep.tile([P, M_BANKS, PACK], F32, name="fade_sb")
         ident = keep.tile([P, P], F32, name="ident")
-        placed = [keep.tile([P, M], F32, name=f"placed{c}") for c in range(E_TILES)]
+        placed = [keep.tile([P, M], F32, name=f"placed{c}") for c in range(WINDOWS)]
 
         nc.vector.memset(key_bytes[:].bitcast(I32), 0)
         make_identity(nc, ident[:])
         nc.gpsimd.dma_start(factor_sb[:], slot_factor[0].rearrange("(p t) -> p t", t=PACK))
         nc.gpsimd.dma_start(fade_sb[:], fade[0].rearrange("(b p j) -> p b j", b=M_BANKS, j=PACK))
 
-        nc.sync.dma_start(tok_list[:], offs)
         nc.sync.dma_start(earl_list[:], offs2)
         nc.sync.dma_start(earl_sb[0][:], earl[0:P, :])
+        nc.sync.dma_start(earl_sb[1][:], earl[P : 2 * P, :])
+        nc.sync.dma_start(tok_list[:], offs)
+        nc.sync.dma_start(q_raw[:], query.rearrange("(p j) q -> p j q", j=PACK))
+        nc.sync.dma_start(key_words[:].bitcast(I32), keys_words[0].rearrange("p n t -> p (n t)").bitcast(I32))
         for quad in range(4):
             nc.scalar.dma_start(
                 key_bytes[32 * quad : 32 * quad + 4, :].bitcast(I32),
                 keys_scales[0, 4 * quad : 4 * quad + 4, :].bitcast(I32),
             )
-        nc.sync.dma_start(key_words[:].bitcast(I32), keys_words[0].rearrange("p n t -> p (n t)").bitcast(I32))
-        nc.sync.dma_start(earl_sb[1][:], earl[P : 2 * P, :])
-        for h in range(Q_TILES):
-            nc.sync.dma_start(q_raw[h][:], query.rearrange("(p j) q -> p j q", j=PACK)[:, :, h * P : (h + 1) * P])
-        nc.sync.dma_start(vals_sb[0][:], vals[0:P, :])
-        nc.sync.dma_start(col_list[:], offs3)
         for kind, c in LOADS:
-            if kind == "v":
+            if kind == "l":
+                nc.sync.dma_start(col_list[:], offs3)
+            elif kind == "v":
                 nc.sync.dma_start(vals_sb[c][:], vals[c * P : (c + 1) * P, :])
             else:
                 nc.sync.dma_start(old_sb[c][:], old[c * P : (c + 1) * P, :])
 
-        for c in range(E_TILES):
+        for c in range(WINDOWS):
             nc.vector.memset(placed[c][:], 0.0)
 
         kg_words = keep.tile([P, I], U32, name="kg_words", align_bytes=64)
@@ -106,7 +106,7 @@ def tile_attend_earliertable_written_lean_kernel(
         q_scales = keep.tile([P, Q], U8, name="q_scales", align_bytes=64)
         for h in range(Q_TILES):
             rows = slice(h * P, (h + 1) * P)
-            nc.vector.tensor_copy(q_bf[:, rows, :], q_raw[h][:].rearrange("p j q -> p q j"))
+            nc.vector.tensor_copy(q_bf[:, rows, :], q_raw[:, :, rows].rearrange("p j q -> p q j"))
             nc.vector.quantize_mx(
                 out=q_codes[:, rows].bitcast(FP8X4), scales=q_scales[:, rows], in_=q_bf[:, rows, :].rearrange("p q j -> p (q j)")
             )
@@ -180,7 +180,7 @@ def tile_attend_earliertable_written_lean_kernel(
             )
             o_sb = keep.tile([P, Q], F32, name=f"o_sb{c}", tag=OTAG[c], align_bytes=64)
             copy_on(OC[c], o_sb[:], o_ps[:])
-            indirect_on(SC[c], placed[c][:].indirect(col_list[:]), o_sb[:])
+            indirect_on(SC[c], placed[c % WINDOWS][:].indirect(col_list[:]), o_sb[:])
 
         def fading(c):
             for b in range(M_BANKS):
@@ -195,13 +195,11 @@ def tile_attend_earliertable_written_lean_kernel(
         def finish(c):
             result = keep.tile([P, M], F32, name=f"result{c}", tag=RTAG[c], align_bytes=64)
             eng = nc.gpsimd if ADDE[c] == "G" else nc.vector
-            for b in range(M_BANKS):
-                cols = slice(b * BANK, (b + 1) * BANK)
-                eng.tensor_tensor(result[:, cols], faded[c][:, cols], placed[c][:, cols], ADD)
-                if c in SPLIT:
-                    nc.sync.dma_start(out[c * P : (c + 1) * P, cols], result[:, cols])
-            if c not in SPLIT:
-                nc.sync.dma_start(out[c * P : (c + 1) * P, :], result[:])
+            width = M // PIECES[c]
+            for k in range(PIECES[c]):
+                cols = slice(k * width, (k + 1) * width)
+                eng.tensor_tensor(result[:, cols], faded[c][:, cols], placed[c % WINDOWS][:, cols], ADD)
+                nc.sync.dma_start(out[c * P : (c + 1) * P, cols], result[:, cols])
 
         steps = {"A": values, "B": product, "M": fading, "C": finish}
         for kind, c in TEXT:

@@ -31,7 +31,7 @@ SC = "SSSS"
 ADDE = "VVVV"
 OTAG = ["vals1","vals2","vals3","o3"]
 RTAG = ["r0","r1","r2","r3"]
-PIECES = [1,1,2,2]
+PIECES = [1,1,2,4]
 
 WINDOWS = 2
 FLOPS = 2 * D * Q * I + 2 * I * E * Q
@@ -49,9 +49,9 @@ def tile_attend_earliertable_written_lean_kernel(
         earl_list = keep.tile([P, I // 16], U16, name="earl_list")
         col_list = keep.tile([P, Q // 16], U16, name="col_list")
         key_words = keep.tile([P, T], U32, name="key_words")
-        key_bytes = keep.tile([P, T], U8, name="key_bytes")
+        key_bytes = keep.tile([P, T], U8, name="key_bytes", tag="key_bytes", align_bytes=64)
         q_raw = keep.tile([P, PACK, Q], F32, name="q_raw")
-        earl_sb = [keep.tile([P, Z], F32, name=f"earl_sb{h}") for h in range(Q_TILES)]
+        earl_sb = [keep.tile([P, Z], F32, name=f"earl_sb{h}", tag=f"earl{h}") for h in range(Q_TILES)]
         vals_sb = [keep.tile([P, T], F32, name=f"vals_sb{c}", tag=f"vals{c}", align_bytes=64) for c in range(E_TILES)]
         old_sb = [keep.tile([P, M], F32, name=f"old_sb{c}") for c in range(E_TILES)]
         factor_sb = keep.tile([P, PACK], F32, name="factor_sb")
@@ -60,21 +60,21 @@ def tile_attend_earliertable_written_lean_kernel(
         placed = [keep.tile([P, M], F32, name=f"placed{c}") for c in range(WINDOWS)]
 
         nc.vector.memset(key_bytes[:].bitcast(I32), 0)
-        make_identity(nc, ident[:])
-        nc.gpsimd.dma_start(factor_sb[:], slot_factor[0].rearrange("(p t) -> p t", t=PACK))
-        nc.gpsimd.dma_start(fade_sb[:], fade[0].rearrange("(b p j) -> p b j", b=M_BANKS, j=PACK))
-
-        nc.sync.dma_start(earl_list[:], offs2)
-        nc.sync.dma_start(earl_sb[0][:], earl[0:P, :])
-        nc.sync.dma_start(earl_sb[1][:], earl[P : 2 * P, :])
-        nc.sync.dma_start(tok_list[:], offs)
-        nc.sync.dma_start(q_raw[:], query.rearrange("(p j) q -> p j q", j=PACK))
-        nc.sync.dma_start(key_words[:].bitcast(I32), keys_words[0].rearrange("p n t -> p (n t)").bitcast(I32))
         for quad in range(4):
             nc.scalar.dma_start(
                 key_bytes[32 * quad : 32 * quad + 4, :].bitcast(I32),
                 keys_scales[0, 4 * quad : 4 * quad + 4, :].bitcast(I32),
             )
+        make_identity(nc, ident[:])
+
+        nc.sync.dma_start(earl_list[:], offs2)
+        nc.scalar.dma_start(fade_sb[:], fade[0].rearrange("(b p j) -> p b j", b=M_BANKS, j=PACK))
+        nc.scalar.dma_start(factor_sb[:], slot_factor[0].rearrange("(p t) -> p t", t=PACK))
+        nc.sync.dma_start(tok_list[:], offs)
+        nc.sync.dma_start(earl_sb[0][:], earl[0:P, :])
+        nc.sync.dma_start(earl_sb[1][:], earl[P : 2 * P, :])
+        nc.sync.dma_start(q_raw[:], query.rearrange("(p j) q -> p j q", j=PACK))
+        nc.sync.dma_start(key_words[:].bitcast(I32), keys_words[0].rearrange("p n t -> p (n t)").bitcast(I32))
         for kind, c in LOADS:
             if kind == "l":
                 nc.sync.dma_start(col_list[:], offs3)
@@ -86,20 +86,29 @@ def tile_attend_earliertable_written_lean_kernel(
         for c in range(WINDOWS):
             nc.vector.memset(placed[c][:], 0.0)
 
-        kg_words = keep.tile([P, I], U32, name="kg_words", align_bytes=64)
+        fade_ps = [psum.tile([P, PACK, P], F32, name=f"fade_ps{b}") for b in range(M_BANKS)]
+        for b in range(M_BANKS):
+            for j in range(PACK):
+                nc.tensor.transpose(fade_ps[b][:, j, :], fade_sb[:, b, j : j + 1].to_broadcast([P, P]), ident[:])
+
         kg_bytes = keep.tile([P, I], U8, name="kg_bytes", align_bytes=64)
         nc.vector.tensor_copy(kg_bytes[:].rearrange("p (t s) -> p s t", t=PACK), key_bytes[:].indirect(tok_list[:]))
+        kg_words = keep.tile([P, I], U32, name="kg_words", tag="key_bytes", align_bytes=64)
         nc.vector.tensor_copy(kg_words[:].rearrange("p (t s) -> p s t", t=PACK), key_words[:].indirect(tok_list[:]))
 
-        gain = keep.tile([P, Q_TILES, PACK, P], F32, name="gain")
+        egs = []
         for h in range(Q_TILES):
             eg = keep.tile([P, I], F32, name=f"eg{h}")
             nc.scalar.activation(eg[:], earl_sb[h][:].indirect(earl_list[:]), COPY)
+            egs.append(eg)
+        gain = [keep.tile([P, PACK, P], F32, name=f"gain{h}", tag=f"earl{1 - h}") for h in range(Q_TILES)]
+        for h in range(Q_TILES):
+            eg = egs[h]
             turned = psum.tile([P, PACK, P], F32, name="turned", tag=f"turn{h}")
             for t in range(PACK):
                 nc.tensor.transpose(turned[:, t, :], eg[:, t::PACK], ident[:])
             for t in range(PACK):
-                nc.scalar.activation(gain[:, h, t, :], turned[:, t, :], COPY, scale=factor_sb[:, t : t + 1])
+                nc.scalar.activation(gain[h][:, t, :], turned[:, t, :], COPY, scale=factor_sb[:, t : t + 1])
 
         q_bf = keep.tile([P, Q, PACK], BF16, name="q_bf", align_bytes=64)
         q_codes = keep.tile([P, Q], U32, name="q_codes", align_bytes=64)
@@ -129,14 +138,9 @@ def tile_attend_earliertable_written_lean_kernel(
                     stop=True,
                 )
             nc.vector.tensor_tensor(
-                w_bf[:, rows, :], scores[:].rearrange("p t q -> p q t"), gain[:, h].rearrange("p t q -> p q t"), MULT
+                w_bf[:, rows, :], scores[:].rearrange("p t q -> p q t"), gain[h][:].rearrange("p t q -> p q t"), MULT
             )
         nc.vector.quantize_mx(out=w_codes[:].bitcast(FP8X4), scales=w_scales[:], in_=w_bf[:].rearrange("p q j -> p (q j)"))
-
-        fade_ps = [psum.tile([P, PACK, P], F32, name=f"fade_ps{b}") for b in range(M_BANKS)]
-        for b in range(M_BANKS):
-            for j in range(PACK):
-                nc.tensor.transpose(fade_ps[b][:, j, :], fade_sb[:, b, j : j + 1].to_broadcast([P, P]), ident[:])
 
         v_codes = [keep.tile([P, P], U32, name=f"v_codes{c}", align_bytes=64) for c in range(E_TILES)]
         v_scales = [keep.tile([P, P], U8, name=f"v_scales{c}", align_bytes=64) for c in range(E_TILES)]

from contextlib import ExitStack

import concourse.mybir as mybir
from concourse.masks import make_identity

F32 = mybir.dt.float32
BF16 = mybir.dt.bfloat16
U32 = mybir.dt.uint32
I32 = mybir.dt.int32
U16 = mybir.dt.uint16
U8 = mybir.dt.uint8
FP8X4 = mybir.dt.float8_e4m3fn_x4
MULT = mybir.AluOpType.mult
ADD = mybir.AluOpType.add
COPY = mybir.ActivationFunctionType.Copy

D, T, I, Q, E, Z, M = 512, 2048, 512, 256, 512, 1024, 1024
P = 128
PACK = 4
BANK = 512
Q_TILES = Q // P
E_TILES = E // P
M_BANKS = M // BANK

LOADS = (("v", 0), ("v", 1), ("l", 0), ("o", 0), ("v", 2), ("o", 1), ("v", 3), ("o", 2), ("o", 3),)
TEXT = (("A", 0), ("A", 1), ("B", 0), ("M", 0), ("A", 2), ("B", 1), ("C", 0), ("A", 3), ("B", 2), ("M", 1), ("C", 1), ("B", 3), ("M", 2), ("C", 2), ("M", 3), ("C", 3),)
VG = "SSSS"
VBF = "VVVV"
OC = "SSSS"
SC = "SSSS"
ADDE = "VVVV"
OTAG = ["vals1","vals2","vals3","o3"]
RTAG = ["r0","r1","r2","r3"]
PIECES = [1,1,2,4]

WINDOWS = 2
FLOPS = 2 * D * Q * I + 2 * I * E * Q


def tile_attend_earliertable_written_lean_kernel(
    tc, query, keys_words, keys_scales, earl, slot_factor, vals, old, fade, offs, offs2, offs3, out
):
    nc = tc.nc
    with ExitStack() as ctx:
        keep = ctx.enter_context(tc.tile_pool(name="keep", bufs=1))
        psum = ctx.enter_context(tc.psum_pool(name="psum", bufs=1))

        tok_list = keep.tile([P, I // 16], U16, name="tok_list")
        earl_list = keep.tile([P, I // 16], U16, name="earl_list")
        col_list = keep.tile([P, Q // 16], U16, name="col_list")
        key_words = keep.tile([P, T], U32, name="key_words")
        key_bytes = keep.tile([P, T], U8, name="key_bytes", tag="key_bytes", align_bytes=64)
        q_raw = keep.tile([P, PACK, Q], F32, name="q_raw")
        earl_sb = [keep.tile([P, Z], F32, name=f"earl_sb{h}", tag=f"earl{h}") for h in range(Q_TILES)]
        vals_sb = [keep.tile([P, T], F32, name=f"vals_sb{c}", tag=f"vals{c}", align_bytes=64) for c in range(E_TILES)]
        old_sb = [keep.tile([P, M], F32, name=f"old_sb{c}") for c in range(E_TILES)]
        factor_sb = keep.tile([P, PACK], F32, name="factor_sb")
        fade_sb = keep.tile([P, M_BANKS, PACK], F32, name="fade_sb")
        ident = keep.tile([P, P], F32, name="ident")
        placed = [keep.tile([P, M], F32, name=f"placed{c}") for c in range(WINDOWS)]

        nc.vector.memset(key_bytes[:].bitcast(I32), 0)
        for quad in range(4):
            nc.scalar.dma_start(
                key_bytes[32 * quad : 32 * quad + 4, :].bitcast(I32),
                keys_scales[0, 4 * quad : 4 * quad + 4, :].bitcast(I32),
            )
        make_identity(nc, ident[:])

        nc.sync.dma_start(earl_list[:], offs2)
        nc.scalar.dma_start(fade_sb[:], fade[0].rearrange("(b p j) -> p b j", b=M_BANKS, j=PACK))
        nc.scalar.dma_start(factor_sb[:], slot_factor[0].rearrange("(p t) -> p t", t=PACK))
        nc.sync.dma_start(tok_list[:], offs)
        nc.sync.dma_start(earl_sb[0][:], earl[0:P, :])
        nc.sync.dma_start(earl_sb[1][:], earl[P : 2 * P, :])
        nc.sync.dma_start(q_raw[:], query.rearrange("(p j) q -> p j q", j=PACK))
        nc.sync.dma_start(key_words[:].bitcast(I32), keys_words[0].rearrange("p n t -> p (n t)").bitcast(I32))
        for kind, c in LOADS:
            if kind == "l":
                nc.sync.dma_start(col_list[:], offs3)
            elif kind == "v":
                nc.sync.dma_start(vals_sb[c][:], vals[c * P : (c + 1) * P, :])
            else:
                nc.sync.dma_start(old_sb[c][:], old[c * P : (c + 1) * P, :])

        for c in range(WINDOWS):
            nc.vector.memset(placed[c][:], 0.0)

        fade_ps = [psum.tile([P, PACK, P], F32, name=f"fade_ps{b}") for b in range(M_BANKS)]
        for b in range(M_BANKS):
            for j in range(PACK):
                nc.tensor.transpose(fade_ps[b][:, j, :], fade_sb[:, b, j : j + 1].to_broadcast([P, P]), ident[:])

        kg_bytes = keep.tile([P, I], U8, name="kg_bytes", align_bytes=64)
        nc.vector.tensor_copy(kg_bytes[:].rearrange("p (t s) -> p s t", t=PACK), key_bytes[:].indirect(tok_list[:]))
        kg_words = keep.tile([P, I], U32, name="kg_words", tag="key_bytes", align_bytes=64)
        nc.vector.tensor_copy(kg_words[:].rearrange("p (t s) -> p s t", t=PACK), key_words[:].indirect(tok_list[:]))

        egs = []
        for h in range(Q_TILES):
            eg = keep.tile([P, I], F32, name=f"eg{h}")
            nc.scalar.activation(eg[:], earl_sb[h][:].indirect(earl_list[:]), COPY)
            egs.append(eg)
        gain = [keep.tile([P, PACK, P], F32, name=f"gain{h}", tag=f"earl{1 - h}") for h in range(Q_TILES)]
        for h in range(Q_TILES):
            eg = egs[h]
            turned = psum.tile([P, PACK, P], F32, name="turned", tag=f"turn{h}")
            for t in range(PACK):
                nc.tensor.transpose(turned[:, t, :], eg[:, t::PACK], ident[:])
            for t in range(PACK):
                nc.scalar.activation(gain[h][:, t, :], turned[:, t, :], COPY, scale=factor_sb[:, t : t + 1])

        q_bf = keep.tile([P, Q, PACK], BF16, name="q_bf", align_bytes=64)
        q_codes = keep.tile([P, Q], U32, name="q_codes", align_bytes=64)
        q_scales = keep.tile([P, Q], U8, name="q_scales", align_bytes=64)
        for h in range(Q_TILES):
            rows = slice(h * P, (h + 1) * P)
            nc.vector.tensor_copy(q_bf[:, rows, :], q_raw[:, :, rows].rearrange("p j q -> p q j"))
            nc.vector.quantize_mx(
                out=q_codes[:, rows].bitcast(FP8X4), scales=q_scales[:, rows], in_=q_bf[:, rows, :].rearrange("p q j -> p (q j)")
            )

        w_bf = keep.tile([P, Q, PACK], BF16, name="w_bf", align_bytes=64)
        w_codes = keep.tile([P, Q], U32, name="w_codes", align_bytes=64)
        w_scales = keep.tile([P, Q], U8, name="w_scales", align_bytes=64)
        for h in range(Q_TILES):
            rows = slice(h * P, (h + 1) * P)
            scores = psum.tile([P, PACK, P], F32, name="scores", tag=f"acc{h}")
            for t in range(PACK):
                cols = slice(t * P, (t + 1) * P)
                nc.tensor.matmul_mx(
                    out=scores[:, t, :],
                    lhsT=kg_words[:, cols].bitcast(FP8X4),
                    lhsT_scale=kg_bytes[:, cols],
                    rhs=q_codes[:, rows].bitcast(FP8X4),
                    rhs_scale=q_scales[:, rows],
                    start=True,
                    stop=True,
                )
            nc.vector.tensor_tensor(
                w_bf[:, rows, :], scores[:].rearrange("p t q -> p q t"), gain[h][:].rearrange("p t q -> p q t"), MULT
            )
        nc.vector.quantize_mx(out=w_codes[:].bitcast(FP8X4), scales=w_scales[:], in_=w_bf[:].rearrange("p q j -> p (q j)"))

        v_codes = [keep.tile([P, P], U32, name=f"v_codes{c}", align_bytes=64) for c in range(E_TILES)]
        v_scales = [keep.tile([P, P], U8, name=f"v_scales{c}", align_bytes=64) for c in range(E_TILES)]
        faded = [keep.tile([P, M], F32, name=f"faded{c}") for c in range(E_TILES)]

        def copy_on(eng, dst, src):
            if eng == "S":
                nc.scalar.copy(dst, src)
            else:
                nc.vector.tensor_copy(dst, src)

        def indirect_on(eng, dst, src):
            if eng == "S":
                nc.scalar.activation(dst, src, COPY)
            else:
                nc.vector.tensor_copy(dst, src)

        def values(c):
            vg = keep.tile([P, I], BF16, name=f"vg{c}")
            indirect_on(VG[c], vg[:], vals_sb[c][:].indirect(tok_list[:]))
            pairs = vg[:].bitcast(F32)
            v_turned = psum.tile([P, 2, P], F32, name="v_turned", tag=f"turn{c % 2}")
            for u in range(2):
                nc.tensor.transpose(v_turned[:, u, :], pairs[:, u::2], ident[:])
            v_bf = keep.tile([P, P, PACK], BF16, name=f"v_bf{c}", tag=f"v_bf{c}", align_bytes=64)
            copy_on(VBF[c], v_bf[:].bitcast(F32), v_turned[:].rearrange("p u e -> p e u"))
            nc.vector.quantize_mx(
                out=v_codes[c][:].bitcast(FP8X4), scales=v_scales[c][:], in_=v_bf[:].rearrange("p e j -> p (e j)")
            )

        def product(c):
            o_ps = psum.tile([P, Q], F32, name="o_ps", tag=f"acc{c % 2}")
            nc.tensor.matmul_mx(
                out=o_ps[:],
                lhsT=v_codes[c][:].bitcast(FP8X4),
                lhsT_scale=v_scales[c][:],
                rhs=w_codes[:].bitcast(FP8X4),
                rhs_scale=w_scales[:],
                start=True,
                stop=True,
            )
            o_sb = keep.tile([P, Q], F32, name=f"o_sb{c}", tag=OTAG[c], align_bytes=64)
            copy_on(OC[c], o_sb[:], o_ps[:])
            indirect_on(SC[c], placed[c % WINDOWS][:].indirect(col_list[:]), o_sb[:])

        def fading(c):
            for b in range(M_BANKS):
                cols = slice(b * BANK, (b + 1) * BANK)
                nc.vector.tensor_tensor(
                    faded[c][:, cols].rearrange("p (r j) -> p r j", j=PACK),
                    old_sb[c][:, cols].rearrange("p (r j) -> p r j", j=PACK),
                    fade_ps[b][:].rearrange("p j r -> p r j"),
                    MULT,
                )

        def finish(c):
            result = keep.tile([P, M], F32, name=f"result{c}", tag=RTAG[c], align_bytes=64)
            eng = nc.gpsimd if ADDE[c] == "G" else nc.vector
            width = M // PIECES[c]
            for k in range(PIECES[c]):
                cols = slice(k * width, (k + 1) * width)
                eng.tensor_tensor(result[:, cols], faded[c][:, cols], placed[c % WINDOWS][:, cols], ADD)
                nc.sync.dma_start(out[c * P : (c + 1) * P, cols], result[:, cols])

        steps = {"A": values, "B": product, "M": fading, "C": finish}
        for kind, c in TEXT:
            steps[kind](c)
